import numpy as np
import ml_dtypes

BF16 = ml_dtypes.bfloat16


def bf(x):
    return np.asarray(x, np.float32).astype(BF16)


def f32(x):
    return np.asarray(x, np.float32)


def f64(x):
    return np.asarray(x).astype(np.float64)


def striped(idx):
    return np.tile(idx.reshape(-1, 16).T, (8, 1))


S, K, M, N, E, Q = 512, 256, 128, 1024, 8, 128


def gelu_tanh(v):
    return 0.5 * v * (1.0 + np.tanh(np.sqrt(2.0 / np.pi) * (v + 0.044715 * v**3)))


def two_experts():
    first = np.random.permutation(S).reshape(E, S // E)
    return np.concatenate([np.random.permutation(np.concatenate([first[e], first[(e + 1) % E]])) for e in range(E)])


def setup_inputs():
    return {"table": bf(np.random.standard_normal((S, K))), "w": bf(np.random.standard_normal((E, K, M)) / np.sqrt(K)), "b": f32(0.5 * np.random.standard_normal((M, 1))), "offs": striped(two_experts())}


def reference(table, w, b, offs):
    idx = offs[:16].T.reshape(-1)
    x = f64(table)[idx].T
    y = np.concatenate([f64(w)[e].T @ x[:, e * Q : (e + 1) * Q] for e in range(E)], axis=1)
    return gelu_tanh(y + f64(b))

@@ -1,0 +1,62 @@
+import concourse.mybir as mybir
+from concourse.masks import make_identity
+
+BF16, F32, U16 = mybir.dt.bfloat16, mybir.dt.float32, mybir.dt.uint16
+GELU = mybir.ActivationFunctionType.Gelu_apprx_tanh
+
+P = 128
+S, K, M, N, E = 512, 256, 128, 1024, 8
+Q = N // E
+TOKEN_BLOCKS = S // P
+K_BLOCKS = K // P
+BANK = 512
+EXPERTS_IN_BANK = BANK // Q
+
+FLOPS = 2 * K * M * N
+
+
+def tile_gather_matmul_kernel(tc, table, w, b, offs, out):
+    nc = tc.nc
+    with (
+        tc.tile_pool(name="held", bufs=1) as held,
+        tc.psum_pool(name="flip", bufs=1) as flip,
+        tc.psum_pool(name="sums", bufs=1) as sums,
+    ):
+        offsets = held.tile([P, N // 16], U16, name="offsets")
+        nc.sync.dma_start(offsets[:], offs)
+        rows = held.tile([P, TOKEN_BLOCKS, K], BF16, name="rows")
+        nc.sync.dma_start(rows[:], table.rearrange("(t p) k -> p t k", p=P))
+        weights = held.tile([P, E, K_BLOCKS, M], BF16, name="weights")
+        nc.scalar.dma_start(weights[:], w.rearrange("e (c p) m -> p e c m", p=P))
+        bias = held.tile([P, 1], F32, name="bias")
+        nc.scalar.dma_start(bias[:], b)
+
+        identity = held.tile([P, P], BF16, name="identity")
+        make_identity(nc, identity[:])
+
+        windows = []
+        for c in range(K_BLOCKS):
+            flipped = flip.tile([P, S], BF16, name=f"flipped{c}")
+            for t in range(TOKEN_BLOCKS):
+                nc.tensor.transpose(flipped[:, t * P : (t + 1) * P], rows[:, t, c * P : (c + 1) * P], identity[:])
+            window = held.tile([P, S], BF16, name=f"window{c}")
+            nc.vector.tensor_copy(window[:], flipped[:])
+            windows.append(window)
+
+        result = held.tile([P, N], F32, name="result")
+        for h in range(N // BANK):
+            bank = sums.tile([P, BANK], F32, name=f"bank{h}")
+            for i in range(EXPERTS_IN_BANK):
+                e = h * EXPERTS_IN_BANK + i
+                piece = offsets[:, e * (Q // 16) : (e + 1) * (Q // 16)]
+                for c in range(K_BLOCKS):
+                    nc.tensor.matmul(
+                        bank[:, i * Q : (i + 1) * Q],
+                        weights[:, e, c, :],
+                        windows[c][:].indirect(piece),
+                        start=(c == 0),
+                        stop=(c == K_BLOCKS - 1),
+                    )
+            columns = slice(h * BANK, (h + 1) * BANK)
+            nc.scalar.activation(result[:, columns], bank[:], GELU, bias=bias[:, 0:1])
+            nc.sync.dma_start(out[:, columns], result[:, columns])

@@ -10,7 +10,7 @@ Q = N // E
 TOKEN_BLOCKS = S // P
 K_BLOCKS = K // P
 BANK = 512
-EXPERTS_IN_BANK = BANK // Q
+WARM_UP = 4
 
 FLOPS = 2 * K * M * N
 
@@ -19,44 +19,61 @@ def tile_gather_matmul_kernel(tc, table, w, b, offs, out):
     nc = tc.nc
     with (
         tc.tile_pool(name="held", bufs=1) as held,
-        tc.psum_pool(name="flip", bufs=1) as flip,
-        tc.psum_pool(name="sums", bufs=1) as sums,
+        tc.psum_pool(name="flip", bufs=4) as flip,
+        tc.psum_pool(name="sums", bufs=4) as sums,
     ):
+        zeros = held.tile([P, BANK], BF16, name="zeros")
+        nc.vector.memset(zeros[:], 0.0)
+        idle_product = sums.tile([P, BANK], F32, name="idle_product", tag="product")
+        for i in range(WARM_UP):
+            nc.tensor.matmul(idle_product[:], zeros[:, 0:P], zeros[:], start=True, stop=True)
+
+        queues = [nc.scalar, nc.sync]
         offsets = held.tile([P, N // 16], U16, name="offsets")
+        rows = []
+        for t in range(TOKEN_BLOCKS):
+            block = held.tile([P, K], BF16, name=f"rows{t}")
+            queues[t % 2].dma_start(block[:], table[t * P : (t + 1) * P, :])
+            rows.append(block)
         nc.sync.dma_start(offsets[:], offs)
-        rows = held.tile([P, TOKEN_BLOCKS, K], BF16, name="rows")
-        nc.sync.dma_start(rows[:], table.rearrange("(t p) k -> p t k", p=P))
-        weights = held.tile([P, E, K_BLOCKS, M], BF16, name="weights")
-        nc.scalar.dma_start(weights[:], w.rearrange("e (c p) m -> p e c m", p=P))
         bias = held.tile([P, 1], F32, name="bias")
-        nc.scalar.dma_start(bias[:], b)
+        nc.sync.dma_start(bias[:], b)
+        weights = []
+        for h in range(2):
+            half = held.tile([P, E // 2, K_BLOCKS, M], BF16, name=f"weights{h}")
+            queues[h].dma_start(half[:], w[h * (E // 2) : (h + 1) * (E // 2)].rearrange("e (c p) m -> p e c m", p=P))
+            weights.append(half)
+
+        scratch = held.tile([P, 1], F32, name="scratch")
+        nc.vector.memset(scratch[:], 0.0)
+        nc.scalar.activation(scratch[:], scratch[:], GELU)
 
         identity = held.tile([P, P], BF16, name="identity")
         make_identity(nc, identity[:])
 
-        windows = []
-        for c in range(K_BLOCKS):
-            flipped = flip.tile([P, S], BF16, name=f"flipped{c}")
-            for t in range(TOKEN_BLOCKS):
-                nc.tensor.transpose(flipped[:, t * P : (t + 1) * P], rows[:, t, c * P : (c + 1) * P], identity[:])
-            window = held.tile([P, S], BF16, name=f"window{c}")
-            nc.vector.tensor_copy(window[:], flipped[:])
-            windows.append(window)
+        windows = [held.tile([P, S], BF16, name=f"window{c}") for c in range(K_BLOCKS)]
+        for t in range(TOKEN_BLOCKS):
+            tokens = slice(t * P, (t + 1) * P)
+            for c in range(K_BLOCKS):
+                flipped = flip.tile([P, P], BF16, name="flipped")
+                nc.tensor.transpose(flipped[:], rows[t][:, c * P : (c + 1) * P], identity[:])
+                if c == 0:
+                    nc.vector.tensor_copy(windows[c][:, tokens], flipped[:])
+                else:
+                    nc.scalar.copy(windows[c][:, tokens], flipped[:])
 
         result = held.tile([P, N], F32, name="result")
-        for h in range(N // BANK):
-            bank = sums.tile([P, BANK], F32, name=f"bank{h}")
-            for i in range(EXPERTS_IN_BANK):
-                e = h * EXPERTS_IN_BANK + i
-                piece = offsets[:, e * (Q // 16) : (e + 1) * (Q // 16)]
-                for c in range(K_BLOCKS):
-                    nc.tensor.matmul(
-                        bank[:, i * Q : (i + 1) * Q],
-                        weights[:, e, c, :],
-                        windows[c][:].indirect(piece),
-                        start=(c == 0),
-                        stop=(c == K_BLOCKS - 1),
-                    )
-            columns = slice(h * BANK, (h + 1) * BANK)
-            nc.scalar.activation(result[:, columns], bank[:], GELU, bias=bias[:, 0:1])
+        for e in range(E):
+            piece = offsets[:, e * (Q // 16) : (e + 1) * (Q // 16)]
+            product = sums.tile([P, Q], F32, name="product")
+            for c in range(K_BLOCKS):
+                nc.tensor.matmul(
+                    product[:],
+                    weights[e // (E // 2)][:, e % (E // 2), c, :],
+                    windows[c][:].indirect(piece),
+                    start=(c == 0),
+                    stop=(c == K_BLOCKS - 1),
+                )
+            columns = slice(e * Q, (e + 1) * Q)
+            nc.scalar.activation(result[:, columns], product[:], GELU, bias=bias[:, 0:1])
             nc.sync.dma_start(out[:, columns], result[:, columns])

@@ -9,8 +9,6 @@ S, K, M, N, E = 512, 256, 128, 1024, 8
 Q = N // E
 TOKEN_BLOCKS = S // P
 K_BLOCKS = K // P
-BANK = 512
-WARM_UP = 4
 
 FLOPS = 2 * K * M * N
 
@@ -19,30 +17,23 @@ def tile_gather_matmul_kernel(tc, table, w, b, offs, out):
     nc = tc.nc
     with (
         tc.tile_pool(name="held", bufs=1) as held,
-        tc.psum_pool(name="flip", bufs=4) as flip,
+        tc.psum_pool(name="flip", bufs=1) as flip,
         tc.psum_pool(name="sums", bufs=4) as sums,
     ):
-        zeros = held.tile([P, BANK], BF16, name="zeros")
-        nc.vector.memset(zeros[:], 0.0)
-        idle_product = sums.tile([P, BANK], F32, name="idle_product", tag="product")
-        for i in range(WARM_UP):
-            nc.tensor.matmul(idle_product[:], zeros[:, 0:P], zeros[:], start=True, stop=True)
-
-        queues = [nc.scalar, nc.sync]
+        halves = []
+        for h, queue in enumerate((nc.sync, nc.scalar)):
+            half = held.tile([P, TOKEN_BLOCKS // 2, K], BF16, name=f"rows{h}")
+            queue.dma_start(half[:], table[h * (S // 2) : (h + 1) * (S // 2), :].rearrange("(t p) k -> p t k", p=P))
+            halves.append(half)
         offsets = held.tile([P, N // 16], U16, name="offsets")
-        rows = []
-        for t in range(TOKEN_BLOCKS):
-            block = held.tile([P, K], BF16, name=f"rows{t}")
-            queues[t % 2].dma_start(block[:], table[t * P : (t + 1) * P, :])
-            rows.append(block)
         nc.sync.dma_start(offsets[:], offs)
         bias = held.tile([P, 1], F32, name="bias")
-        nc.sync.dma_start(bias[:], b)
+        nc.scalar.dma_start(bias[:], b)
         weights = []
-        for h in range(2):
-            half = held.tile([P, E // 2, K_BLOCKS, M], BF16, name=f"weights{h}")
-            queues[h].dma_start(half[:], w[h * (E // 2) : (h + 1) * (E // 2)].rearrange("e (c p) m -> p e c m", p=P))
-            weights.append(half)
+        for pair in range(E // 2):
+            two = held.tile([P, 2, K_BLOCKS, M], BF16, name=f"weights{pair}")
+            nc.sync.dma_start(two[:], w[2 * pair : 2 * pair + 2].rearrange("e (c p) m -> p e c m", p=P))
+            weights.append(two)
 
         scratch = held.tile([P, 1], F32, name="scratch")
         nc.vector.memset(scratch[:], 0.0)
@@ -51,29 +42,30 @@ def tile_gather_matmul_kernel(tc, table, w, b, offs, out):
         identity = held.tile([P, P], BF16, name="identity")
         make_identity(nc, identity[:])
 
-        windows = [held.tile([P, S], BF16, name=f"window{c}") for c in range(K_BLOCKS)]
-        for t in range(TOKEN_BLOCKS):
-            tokens = slice(t * P, (t + 1) * P)
-            for c in range(K_BLOCKS):
-                flipped = flip.tile([P, P], BF16, name="flipped")
-                nc.tensor.transpose(flipped[:], rows[t][:, c * P : (c + 1) * P], identity[:])
-                if c == 0:
-                    nc.vector.tensor_copy(windows[c][:, tokens], flipped[:])
-                else:
-                    nc.scalar.copy(windows[c][:, tokens], flipped[:])
+        windows = []
+        for c in range(K_BLOCKS):
+            flipped = flip.tile([P, S], BF16, name=f"flipped{c}")
+            for t in range(TOKEN_BLOCKS):
+                block = halves[t // 2][:, t % 2, c * P : (c + 1) * P]
+                nc.tensor.transpose(flipped[:, t * P : (t + 1) * P], block, identity[:])
+            window = held.tile([P, S], BF16, name=f"window{c}")
+            nc.vector.tensor_copy(window[:], flipped[:])
+            windows.append(window)
 
         result = held.tile([P, N], F32, name="result")
-        for e in range(E):
-            piece = offsets[:, e * (Q // 16) : (e + 1) * (Q // 16)]
-            product = sums.tile([P, Q], F32, name="product")
+        for pair in range(E // 2):
+            products = [sums.tile([P, Q], F32, name="product") for i in range(2)]
             for c in range(K_BLOCKS):
-                nc.tensor.matmul(
-                    product[:],
-                    weights[e // (E // 2)][:, e % (E // 2), c, :],
-                    windows[c][:].indirect(piece),
-                    start=(c == 0),
-                    stop=(c == K_BLOCKS - 1),
-                )
-            columns = slice(e * Q, (e + 1) * Q)
-            nc.scalar.activation(result[:, columns], product[:], GELU, bias=bias[:, 0:1])
-            nc.sync.dma_start(out[:, columns], result[:, columns])
+                for i in range(2):
+                    e = 2 * pair + i
+                    nc.tensor.matmul(
+                        products[i][:],
+                        weights[pair][:, i, c, :],
+                        windows[c][:].indirect(offsets[:, e * (Q // 16) : (e + 1) * (Q // 16)]),
+                        start=(c == 0),
+                        stop=(c == K_BLOCKS - 1),
+                    )
+            for i in range(2):
+                columns = slice((2 * pair + i) * Q, (2 * pair + i + 1) * Q)
+                nc.scalar.activation(result[:, columns], products[i][:], GELU, bias=bias[:, 0:1])
+                nc.sync.dma_start(out[:, columns], result[:, columns])

@@ -9,6 +9,8 @@ S, K, M, N, E = 512, 256, 128, 1024, 8
 Q = N // E
 TOKEN_BLOCKS = S // P
 K_BLOCKS = K // P
+BANK = 512
+WARM_UP = 4
 
 FLOPS = 2 * K * M * N
 
@@ -20,6 +22,12 @@ def tile_gather_matmul_kernel(tc, table, w, b, offs, out):
         tc.psum_pool(name="flip", bufs=1) as flip,
         tc.psum_pool(name="sums", bufs=4) as sums,
     ):
+        zeros = held.tile([P, BANK], BF16, name="zeros")
+        nc.vector.memset(zeros[:], 0.0)
+        idle_product = sums.tile([P, BANK], F32, name="idle_product", tag="product")
+        for i in range(WARM_UP):
+            nc.tensor.matmul(idle_product[:], zeros[:, 0:P], zeros[:], start=True, stop=True)
+
         halves = []
         for h, queue in enumerate((nc.sync, nc.scalar)):
             half = held.tile([P, TOKEN_BLOCKS // 2, K], BF16, name=f"rows{h}")
@@ -48,6 +56,8 @@ def tile_gather_matmul_kernel(tc, table, w, b, offs, out):
             for t in range(TOKEN_BLOCKS):
                 block = halves[t // 2][:, t % 2, c * P : (c + 1) * P]
                 nc.tensor.transpose(flipped[:, t * P : (t + 1) * P], block, identity[:])
+            kept_busy = sums.tile([P, BANK], F32, name="kept_busy", tag="product")
+            nc.tensor.matmul(kept_busy[:], identity[:], halves[c][:, :, :], start=True, stop=True)
             window = held.tile([P, S], BF16, name=f"window{c}")
             nc.vector.tensor_copy(window[:], flipped[:])
             windows.append(window)

@@ -56,8 +56,6 @@ def tile_gather_matmul_kernel(tc, table, w, b, offs, out):
             for t in range(TOKEN_BLOCKS):
                 block = halves[t // 2][:, t % 2, c * P : (c + 1) * P]
                 nc.tensor.transpose(flipped[:, t * P : (t + 1) * P], block, identity[:])
-            kept_busy = sums.tile([P, BANK], F32, name="kept_busy", tag="product")
-            nc.tensor.matmul(kept_busy[:], identity[:], halves[c][:, :, :], start=True, stop=True)
             window = held.tile([P, S], BF16, name=f"window{c}")
             nc.vector.tensor_copy(window[:], flipped[:])
             windows.append(window)

@@ -52,12 +52,13 @@ def tile_gather_matmul_kernel(tc, table, w, b, offs, out):
 
         windows = []
         for c in range(K_BLOCKS):
-            flipped = flip.tile([P, S], BF16, name=f"flipped{c}")
-            for t in range(TOKEN_BLOCKS):
-                block = halves[t // 2][:, t % 2, c * P : (c + 1) * P]
-                nc.tensor.transpose(flipped[:, t * P : (t + 1) * P], block, identity[:])
             window = held.tile([P, S], BF16, name=f"window{c}")
-            nc.vector.tensor_copy(window[:], flipped[:])
+            for h in range(2):
+                flipped = flip.tile([P, S // 2], BF16, name=f"flipped{c}{h}")
+                for t in range(TOKEN_BLOCKS // 2):
+                    block = halves[h][:, t, c * P : (c + 1) * P]
+                    nc.tensor.transpose(flipped[:, t * P : (t + 1) * P], block, identity[:])
+                nc.vector.tensor_copy(window[:, h * (S // 2) : (h + 1) * (S // 2)], flipped[:])
             windows.append(window)
 
         result = held.tile([P, N], F32, name="result")

@@ -30,8 +30,8 @@ def tile_gather_matmul_kernel(tc, table, w, b, offs, out):
 
         halves = []
         for h, queue in enumerate((nc.sync, nc.scalar)):
-            half = held.tile([P, TOKEN_BLOCKS // 2, K], BF16, name=f"rows{h}")
-            queue.dma_start(half[:], table[h * (S // 2) : (h + 1) * (S // 2), :].rearrange("(t p) k -> p t k", p=P))
+            half = held.tile([P, TOKEN_BLOCKS // 2, P, K_BLOCKS], BF16, name=f"rows{h}")
+            queue.dma_start(half[:], table[h * (S // 2) : (h + 1) * (S // 2), :].rearrange("(t p) (f c) -> p t f c", p=P, c=K_BLOCKS))
             halves.append(half)
         offsets = held.tile([P, N // 16], U16, name="offsets")
         nc.sync.dma_start(offsets[:], offs)
@@ -40,7 +40,7 @@ def tile_gather_matmul_kernel(tc, table, w, b, offs, out):
         weights = []
         for pair in range(E // 2):
             two = held.tile([P, 2, K_BLOCKS, M], BF16, name=f"weights{pair}")
-            nc.sync.dma_start(two[:], w[2 * pair : 2 * pair + 2].rearrange("e (c p) m -> p e c m", p=P))
+            nc.sync.dma_start(two[:], w[2 * pair : 2 * pair + 2].rearrange("e (p c) m -> p e c m", p=P))
             weights.append(two)
 
         scratch = held.tile([P, 1], F32, name="scratch")
@@ -56,7 +56,7 @@ def tile_gather_matmul_kernel(tc, table, w, b, offs, out):
             for h in range(2):
                 flipped = flip.tile([P, S // 2], BF16, name=f"flipped{c}{h}")
                 for t in range(TOKEN_BLOCKS // 2):
-                    block = halves[h][:, t, c * P : (c + 1) * P]
+                    block = halves[h][:, t, :, c]
                     nc.tensor.transpose(flipped[:, t * P : (t + 1) * P], block, identity[:])
                 nc.vector.tensor_copy(window[:, h * (S // 2) : (h + 1) * (S // 2)], flipped[:])
             windows.append(window)

@@ -30,8 +30,8 @@ def tile_gather_matmul_kernel(tc, table, w, b, offs, out):
 
         halves = []
         for h, queue in enumerate((nc.sync, nc.scalar)):
-            half = held.tile([P, TOKEN_BLOCKS // 2, P, K_BLOCKS], BF16, name=f"rows{h}")
-            queue.dma_start(half[:], table[h * (S // 2) : (h + 1) * (S // 2), :].rearrange("(t p) (f c) -> p t f c", p=P, c=K_BLOCKS))
+            half = held.tile([P, TOKEN_BLOCKS // 2, K], BF16, name=f"rows{h}")
+            queue.dma_start(half[:], table[h * (S // 2) : (h + 1) * (S // 2), :].rearrange("(t p) k -> p t k", p=P))
             halves.append(half)
         offsets = held.tile([P, N // 16], U16, name="offsets")
         nc.sync.dma_start(offsets[:], offs)
@@ -47,19 +47,25 @@ def tile_gather_matmul_kernel(tc, table, w, b, offs, out):
         nc.vector.memset(scratch[:], 0.0)
         nc.scalar.activation(scratch[:], scratch[:], GELU)
 
-        identity = held.tile([P, P], BF16, name="identity")
+        identity = held.tile([P, P], F32, name="identity")
         make_identity(nc, identity[:])
 
-        windows = []
+        flipped = []
+        for block in range(TOKEN_BLOCKS):
+            words = halves[block // 2][:, block % 2, :].bitcast(F32)
+            pairs = flip.tile([P, P], F32, name=f"pairs{block}")
+            nc.tensor.transpose(pairs[:], words, identity[:])
+            flipped.append(pairs)
+
+        windows = [held.tile([P, S], BF16, name=f"window{c}") for c in range(K_BLOCKS)]
         for c in range(K_BLOCKS):
-            window = held.tile([P, S], BF16, name=f"window{c}")
-            for h in range(2):
-                flipped = flip.tile([P, S // 2], BF16, name=f"flipped{c}{h}")
-                for t in range(TOKEN_BLOCKS // 2):
-                    block = halves[h][:, t, :, c]
-                    nc.tensor.transpose(flipped[:, t * P : (t + 1) * P], block, identity[:])
-                nc.vector.tensor_copy(window[:, h * (S // 2) : (h + 1) * (S // 2)], flipped[:])
-            windows.append(window)
+            for block in range(TOKEN_BLOCKS):
+                feature_c = flipped[block][:].bitcast(BF16).rearrange("p (s c) -> p s c", c=K_BLOCKS)[:, :, c]
+                columns = windows[c][:, block * P : (block + 1) * P]
+                if block % 2 == 0:
+                    nc.vector.tensor_copy(columns, feature_c)
+                else:
+                    nc.scalar.copy(columns, feature_c)
 
         result = held.tile([P, N], F32, name="result")
         for pair in range(E // 2):

@@ -10,7 +10,7 @@ Q = N // E
 TOKEN_BLOCKS = S // P
 K_BLOCKS = K // P
 BANK = 512
-WARM_UP = 4
+WARM_UP = 3
 
 FLOPS = 2 * K * M * N
 
@@ -56,6 +56,8 @@ def tile_gather_matmul_kernel(tc, table, w, b, offs, out):
             pairs = flip.tile([P, P], F32, name=f"pairs{block}")
             nc.tensor.transpose(pairs[:], words, identity[:])
             flipped.append(pairs)
+
+        nc.tensor.matmul(idle_product[:, 0:P], identity[:], halves[1][:, 1, :].bitcast(F32), start=True, stop=True)
 
         windows = [held.tile([P, S], BF16, name=f"window{c}") for c in range(K_BLOCKS)]
         for c in range(K_BLOCKS):

import concourse.mybir as mybir
from concourse.masks import make_identity

BF16, F32, U16 = mybir.dt.bfloat16, mybir.dt.float32, mybir.dt.uint16
GELU = mybir.ActivationFunctionType.Gelu_apprx_tanh

P = 128
S, K, M, N, E = 512, 256, 128, 1024, 8
Q = N // E
TOKEN_BLOCKS = S // P
K_BLOCKS = K // P
BANK = 512
WARM_UP = 3

FLOPS = 2 * K * M * N


def tile_gather_matmul_kernel(tc, table, w, b, offs, out):
    nc = tc.nc
    with (
        tc.tile_pool(name="held", bufs=1) as held,
        tc.psum_pool(name="flip", bufs=1) as flip,
        tc.psum_pool(name="sums", bufs=4) as sums,
    ):
        zeros = held.tile([P, BANK], BF16, name="zeros")
        nc.vector.memset(zeros[:], 0.0)
        idle_product = sums.tile([P, BANK], F32, name="idle_product", tag="product")
        for i in range(WARM_UP):
            nc.tensor.matmul(idle_product[:], zeros[:, 0:P], zeros[:], start=True, stop=True)

        halves = []
        for h, queue in enumerate((nc.sync, nc.scalar)):
            half = held.tile([P, TOKEN_BLOCKS // 2, K], BF16, name=f"rows{h}")
            queue.dma_start(half[:], table[h * (S // 2) : (h + 1) * (S // 2), :].rearrange("(t p) k -> p t k", p=P))
            halves.append(half)
        offsets = held.tile([P, N // 16], U16, name="offsets")
        nc.sync.dma_start(offsets[:], offs)
        bias = held.tile([P, 1], F32, name="bias")
        nc.scalar.dma_start(bias[:], b)
        weights = []
        for pair in range(E // 2):
            two = held.tile([P, 2, K_BLOCKS, M], BF16, name=f"weights{pair}")
            nc.sync.dma_start(two[:], w[2 * pair : 2 * pair + 2].rearrange("e (p c) m -> p e c m", p=P))
            weights.append(two)

        scratch = held.tile([P, 1], F32, name="scratch")
        nc.vector.memset(scratch[:], 0.0)
        nc.scalar.activation(scratch[:], scratch[:], GELU)

        identity = held.tile([P, P], F32, name="identity")
        make_identity(nc, identity[:])

        flipped = []
        for block in range(TOKEN_BLOCKS):
            words = halves[block // 2][:, block % 2, :].bitcast(F32)
            pairs = flip.tile([P, P], F32, name=f"pairs{block}")
            nc.tensor.transpose(pairs[:], words, identity[:])
            flipped.append(pairs)

        nc.tensor.matmul(idle_product[:, 0:P], identity[:], halves[1][:, 1, :].bitcast(F32), start=True, stop=True)

        windows = [held.tile([P, S], BF16, name=f"window{c}") for c in range(K_BLOCKS)]
        for c in range(K_BLOCKS):
            for block in range(TOKEN_BLOCKS):
                feature_c = flipped[block][:].bitcast(BF16).rearrange("p (s c) -> p s c", c=K_BLOCKS)[:, :, c]
                columns = windows[c][:, block * P : (block + 1) * P]
                if block % 2 == 0:
                    nc.vector.tensor_copy(columns, feature_c)
                else:
                    nc.scalar.copy(columns, feature_c)

        result = held.tile([P, N], F32, name="result")
        for pair in range(E // 2):
            products = [sums.tile([P, Q], F32, name="product") for i in range(2)]
            for c in range(K_BLOCKS):
                for i in range(2):
                    e = 2 * pair + i
                    nc.tensor.matmul(
                        products[i][:],
                        weights[pair][:, i, c, :],
                        windows[c][:].indirect(offsets[:, e * (Q // 16) : (e + 1) * (Q // 16)]),
                        start=(c == 0),
                        stop=(c == K_BLOCKS - 1),
                    )
            for i in range(2):
                columns = slice((2 * pair + i) * Q, (2 * pair + i + 1) * Q)
                nc.scalar.activation(result[:, columns], products[i][:], GELU, bias=bias[:, 0:1])
                nc.sync.dma_start(out[:, columns], result[:, columns])
